import numpy as np, ml_dtypes
CORES = [56,61,80,85]
N = 4
F = 512
def setup_inputs(rng):
    return {"ah": rng.standard_normal((N, 128, 128), dtype=np.float32).astype(ml_dtypes.bfloat16), "al": (rng.standard_normal((N, 128, 128), dtype=np.float32) / 256).astype(ml_dtypes.bfloat16), "bh": rng.standard_normal((N, 128, F), dtype=np.float32).astype(ml_dtypes.bfloat16), "bl": (rng.standard_normal((N, 128, F), dtype=np.float32) / 256).astype(ml_dtypes.bfloat16)}
def setup_inputs_big(rng):
    d = setup_inputs(rng)
    for k in ("ah", "al", "bh", "bl"): d[k] = (d[k].astype(np.float32) * 1024.0).astype(d[k].dtype)
    return d
def setup_inputs_small(rng):
    d = setup_inputs(rng)
    for k in ("ah", "al", "bh", "bl"): d[k] = (d[k].astype(np.float32) * (1 / 1024.0)).astype(d[k].dtype)
    return d
def setup_inputs_apart(rng):
    d = setup_inputs(rng)
    f = (10.0 ** rng.permutation(np.linspace(-1.5, 1.5, N))).astype(np.float32).reshape(N, 1, 1)
    for k in ("ah", "al", "bh", "bl"): d[k] = (d[k].astype(np.float32) * f).astype(d[k].dtype)
    return d
def reference(ah, al, bh, bl):
    AH, AL, BH, BL = ah.astype(np.float64), al.astype(np.float64), bh.astype(np.float64), bl.astype(np.float64)
    s = sum((AH[j] + AL[j]).T @ (BH[j] + BL[j]) for j in range(N))
    s = s.astype(np.float32 if ah.dtype != np.float64 else np.float64)
    return {"y": np.broadcast_to(s, (N,) + s.shape)}

@@ -1,0 +1,157 @@
+from concourse.bass import DstId, RemoteDMATransfer
+from concourse.mybir import AluOpType
+
+NSIM = 96
+F = 512
+NBLK = 4
+BW = F // NBLK
+NHALF = 2
+HW = F // NHALF
+BPH = NBLK // NHALF
+
+SCRATCH = {
+    "ah_s": ("sbuf", [128, 128], "bfloat16"),
+    "al_s": ("sbuf", [128, 128], "bfloat16"),
+    "bh_s": ("sbuf", [128, F], "bfloat16"),
+    "bl_s": ("sbuf", [128, F], "bfloat16"),
+    "ps0": ("psum", [128, 512], "float32"),
+    "ps1": ("psum", [128, 512], "float32"),
+    "part": ("sbuf", [128, F], "float32"),
+    "peer": ("sbuf", [128, F], "float32"),
+    "rem": ("sbuf", [128, F], "float32"),
+    "out": ("sbuf", [128, F], "float32"),
+    "land0": ("sbuf", [128, BW], "float32"),
+    "land1": ("sbuf", [128, BW], "float32"),
+}
+SEMAPHORES = ["lda", "ldb0", "ldb1", "mm0", "mm1", "cp0", "cp1", "sent", "arr", "peer_in", "acc0", "acc1",
+              "rem0", "rem1", "fin0", "fin1", "st"]
+
+
+def _pick(mask, lo, n):
+    bits = [i for i in range(mask.bit_length()) if (mask >> i) & 1]
+    m = 0
+    for b in bits[lo:lo + n]:
+        m |= 1 << b
+    return m
+
+
+def _count(mask):
+    return sum((mask >> i) & 1 for i in range(mask.bit_length()))
+
+
+def _plan(T, topo, chip):
+    local = [c for c in T.cores if topo.chip(c) == chip]
+    far = [c for c in T.cores if topo.chip(c) != chip]
+    by_die = {}
+    for c in range(NSIM):
+        if topo.chip(c) == chip and c not in T.cores and all(topo.may_write(c, d) for d in far):
+            by_die.setdefault(topo.die(c), []).append(c)
+    relays = []
+    for i in range(max(len(v) for v in by_die.values())):
+        for d in sorted(by_die):
+            if i < len(by_die[d]):
+                relays.append(by_die[d][i])
+    return local, far, relays[:NBLK]
+
+
+def _dst(topo, c):
+    rid, pid, _ = topo.addr(c)
+    return DstId(rid=rid, pnc=pid)
+
+
+def _relay(g, core, T, topo, far, q):
+    mask = topo.mask(core, far[0])
+    for d in far[1:]:
+        mask &= topo.mask(core, d)
+    n = _count(mask)
+    cols = slice(q * BW, (q + 1) * BW)
+    g.wait_ge(T.sem.arr, 2 * W1_ENG)
+    g.remote_dma_fused(
+        [RemoteDMATransfer(dst_ids=[_dst(topo, d) for d in far], dma_engine_mask=mask,
+                           remote_sem=T.sem["rem%d" % (q // BPH)],
+                           srcs=[T.land0[:], T.land1[:]], dsts=[T.rem[:, cols] for _ in far], alu_op=1)],
+        local_sem=T.sem.sent)
+    g.wait_ge(T.sem.sent, n)
+
+
+W1_ENG = 8
+
+
+def rank_program(g, core, T, topo):
+    chips = sorted({topo.chip(c) for c in T.cores})
+    if topo.chip(core) not in chips:
+        return
+    local, far, relays = _plan(T, topo, topo.chip(core))
+    if core in relays:
+        _relay(g, core, T, topo, far, relays.index(core))
+        return
+    if T.rank_of(core) is None:
+        return
+    slot = local.index(core)
+    peer = local[1 - slot]
+    ps = [T.ps0, T.ps1]
+    sem = T.sem
+
+    g.sync.dma_start(T.ah_s[:], T.ah[:]).then_inc(sem.lda, 16)
+    g.scalar.dma_start(T.al_s[:], T.al[:]).then_inc(sem.lda, 16)
+    for h in range(NHALF):
+        c = slice(h * HW, (h + 1) * HW)
+        g.sync.dma_start(T.bh_s[:, c], T.bh[:, c]).then_inc(sem["ldb%d" % h], 16)
+        g.scalar.dma_start(T.bl_s[:, c], T.bl[:, c]).then_inc(sem["ldb%d" % h], 16)
+
+    g.tensor.wait_ge(sem.lda, 32)
+    for h in range(NHALF):
+        c = slice(h * HW, (h + 1) * HW)
+        g.tensor.wait_ge(sem["ldb%d" % h], 32)
+        terms = [(T.al_s, T.bl_s), (T.al_s, T.bh_s), (T.ah_s, T.bl_s), (T.ah_s, T.bh_s)]
+        for i, (a, b) in enumerate(terms):
+            g.tensor.matmul(ps[h][:, 0:HW], a[:], b[:, c], start=(i == 0), stop=(i == len(terms) - 1)
+                            ).then_inc(sem["mm%d" % h], 1)
+
+    for h in range(NHALF):
+        c = slice(h * HW, (h + 1) * HW)
+        g.vector.wait_ge(sem["mm%d" % h], 4)
+        g.vector.tensor_copy(T.part[:, c], ps[h][:, 0:HW]).then_inc(sem["cp%d" % h], 1)
+
+    sent = 0
+    for h in range(NHALF):
+        g.wait_ge(sem["cp%d" % h], 1)
+        trs = []
+        for j in range(BPH):
+            q = h * BPH + j
+            r = relays[q]
+            trs.append(RemoteDMATransfer(dst_ids=[_dst(topo, r)],
+                                         dma_engine_mask=_pick(topo.mask(core, r), j * W1_ENG, W1_ENG),
+                                         remote_sem=sem.arr, src=T.part[:, q * BW:(q + 1) * BW],
+                                         dst=T["land%d" % slot][:]))
+            sent += W1_ENG
+        g.remote_dma_fused(trs, local_sem=sem.sent)
+    rid, pid, _ = topo.addr(peer)
+    pmask = topo.mask(core, peer)
+    g.remote_dma(T.peer[:], T.part[:], sem.peer_in, sem.sent, pid, rid, pmask)
+    sent += _count(pmask)
+
+    g.vector.wait_ge(sem.peer_in, _count(topo.mask(peer, core)))
+    for h in range(NHALF):
+        c = slice(h * HW, (h + 1) * HW)
+        g.vector.tensor_tensor(ps[h][:, 0:HW], ps[h][:, 0:HW], T.peer[:, c], AluOpType.add
+                               ).then_inc(sem["acc%d" % h], 1)
+    far_relays = _plan(T, topo, topo.chip(far[0]))[2]
+    stq = [g.sync, g.scalar]
+    for h in range(NHALF):
+        c = slice(h * HW, (h + 1) * HW)
+        n = 0
+        for q in range(h * BPH, (h + 1) * BPH):
+            m = topo.mask(far_relays[q], local[0])
+            for d in local[1:]:
+                m &= topo.mask(far_relays[q], d)
+            n += _count(m)
+        g.vector.wait_ge(sem["acc%d" % h], 1)
+        g.vector.wait_ge(sem["rem%d" % h], n)
+        g.vector.tensor_tensor(T.out[:, c], ps[h][:, 0:HW], T.rem[:, c], AluOpType.add
+                               ).then_inc(sem["fin%d" % h], 1)
+        stq[h].wait_ge(sem["fin%d" % h], 1)
+        stq[h].dma_start(T.y[:, c], T.out[:, c]).then_inc(sem.st, 16)
+
+    g.wait_ge(sem.sent, sent)
+    g.wait_ge(sem.st, 16 * NHALF)

@@ -5,9 +5,9 @@ NSIM = 96
 F = 512
 NBLK = 4
 BW = F // NBLK
-NHALF = 2
-HW = F // NHALF
-BPH = NBLK // NHALF
+HALVES = [[0, 1], [2, 3]]
+CALLS = [[0], [1], [2, 3]]
+W1_ENG = 8
 
 SCRATCH = {
     "ah_s": ("sbuf", [128, 128], "bfloat16"),
@@ -16,6 +16,8 @@ SCRATCH = {
     "bl_s": ("sbuf", [128, F], "bfloat16"),
     "ps0": ("psum", [128, 512], "float32"),
     "ps1": ("psum", [128, 512], "float32"),
+    "ps2": ("psum", [128, 512], "float32"),
+    "ps3": ("psum", [128, 512], "float32"),
     "part": ("sbuf", [128, F], "float32"),
     "peer": ("sbuf", [128, F], "float32"),
     "rem": ("sbuf", [128, F], "float32"),
@@ -23,8 +25,10 @@ SCRATCH = {
     "land0": ("sbuf", [128, BW], "float32"),
     "land1": ("sbuf", [128, BW], "float32"),
 }
-SEMAPHORES = ["lda", "ldb0", "ldb1", "mm0", "mm1", "cp0", "cp1", "sent", "arr", "peer_in", "acc0", "acc1",
-              "rem0", "rem1", "fin0", "fin1", "st"]
+SEMAPHORES = (["lda", "sent", "arr", "peer_in", "acc", "st"]
+              + ["ldh%d" % h for h in range(2)] + ["ldl%d" % h for h in range(2)] + ["fin%d" % h for h in range(2)]
+              + ["mm%d" % q for q in range(NBLK)] + ["cp%d" % q for q in range(NBLK)]
+              + ["rem%d" % q for q in range(NBLK)])
 
 
 def _pick(mask, lo, n):
@@ -54,27 +58,35 @@ def _plan(T, topo, chip):
     return local, far, relays[:NBLK]
 
 
+def _out_mask(topo, src, dsts):
+    m = topo.mask(src, dsts[0])
+    for d in dsts[1:]:
+        m &= topo.mask(src, d)
+    return m
+
+
 def _dst(topo, c):
     rid, pid, _ = topo.addr(c)
     return DstId(rid=rid, pnc=pid)
 
 
+def _cols(q):
+    return slice(q * BW, (q + 1) * BW)
+
+
+def _span(blocks):
+    return slice(blocks[0] * BW, (blocks[-1] + 1) * BW)
+
+
 def _relay(g, core, T, topo, far, q):
-    mask = topo.mask(core, far[0])
-    for d in far[1:]:
-        mask &= topo.mask(core, d)
-    n = _count(mask)
-    cols = slice(q * BW, (q + 1) * BW)
+    mask = _out_mask(topo, core, far)
     g.wait_ge(T.sem.arr, 2 * W1_ENG)
     g.remote_dma_fused(
         [RemoteDMATransfer(dst_ids=[_dst(topo, d) for d in far], dma_engine_mask=mask,
-                           remote_sem=T.sem["rem%d" % (q // BPH)],
-                           srcs=[T.land0[:], T.land1[:]], dsts=[T.rem[:, cols] for _ in far], alu_op=1)],
+                           remote_sem=T.sem["rem%d" % q],
+                           srcs=[T.land0[:], T.land1[:]], dsts=[T.rem[:, _cols(q)] for _ in far], alu_op=1)],
         local_sem=T.sem.sent)
-    g.wait_ge(T.sem.sent, n)
-
-
-W1_ENG = 8
+    g.wait_ge(T.sem.sent, _count(mask))
 
 
 def rank_program(g, core, T, topo):
@@ -89,40 +101,45 @@ def rank_program(g, core, T, topo):
         return
     slot = local.index(core)
     peer = local[1 - slot]
-    ps = [T.ps0, T.ps1]
+    ps = [T.ps0, T.ps1, T.ps2, T.ps3]
     sem = T.sem
 
     g.sync.dma_start(T.ah_s[:], T.ah[:]).then_inc(sem.lda, 16)
     g.scalar.dma_start(T.al_s[:], T.al[:]).then_inc(sem.lda, 16)
-    for h in range(NHALF):
-        c = slice(h * HW, (h + 1) * HW)
-        g.sync.dma_start(T.bh_s[:, c], T.bh[:, c]).then_inc(sem["ldb%d" % h], 16)
-        g.scalar.dma_start(T.bl_s[:, c], T.bl[:, c]).then_inc(sem["ldb%d" % h], 16)
+    for h, blocks in enumerate(HALVES):
+        c = _span(blocks)
+        g.sync.dma_start(T.bh_s[:, c], T.bh[:, c]).then_inc(sem["ldh%d" % h], 16)
+        g.scalar.dma_start(T.bl_s[:, c], T.bl[:, c]).then_inc(sem["ldl%d" % h], 16)
 
     g.tensor.wait_ge(sem.lda, 32)
-    for h in range(NHALF):
-        c = slice(h * HW, (h + 1) * HW)
-        g.tensor.wait_ge(sem["ldb%d" % h], 32)
-        terms = [(T.al_s, T.bl_s), (T.al_s, T.bh_s), (T.ah_s, T.bl_s), (T.ah_s, T.bh_s)]
-        for i, (a, b) in enumerate(terms):
-            g.tensor.matmul(ps[h][:, 0:HW], a[:], b[:, c], start=(i == 0), stop=(i == len(terms) - 1)
-                            ).then_inc(sem["mm%d" % h], 1)
+    for h, blocks in enumerate(HALVES):
+        g.tensor.wait_ge(sem["ldh%d" % h], 16)
+        for q in blocks:
+            g.tensor.matmul(ps[q][:, 0:BW], T.ah_s[:], T.bh_s[:, _cols(q)], start=True, stop=False
+                            ).then_inc(sem["mm%d" % q], 1)
+            g.tensor.matmul(ps[q][:, 0:BW], T.al_s[:], T.bh_s[:, _cols(q)], start=False, stop=False
+                            ).then_inc(sem["mm%d" % q], 1)
+        g.tensor.wait_ge(sem["ldl%d" % h], 16)
+        for q in blocks:
+            g.tensor.matmul(ps[q][:, 0:BW], T.ah_s[:], T.bl_s[:, _cols(q)], start=False, stop=False
+                            ).then_inc(sem["mm%d" % q], 1)
+            g.tensor.matmul(ps[q][:, 0:BW], T.al_s[:], T.bl_s[:, _cols(q)], start=False, stop=True
+                            ).then_inc(sem["mm%d" % q], 1)
 
-    for h in range(NHALF):
-        c = slice(h * HW, (h + 1) * HW)
-        g.vector.wait_ge(sem["mm%d" % h], 4)
-        g.vector.tensor_copy(T.part[:, c], ps[h][:, 0:HW]).then_inc(sem["cp%d" % h], 1)
+    for q in range(NBLK):
+        g.vector.wait_ge(sem["mm%d" % q], 4)
+        g.vector.tensor_copy(T.part[:, _cols(q)], ps[q][:, 0:BW]).then_inc(sem["cp%d" % q], 1)
 
     sent = 0
-    for h in range(NHALF):
-        g.wait_ge(sem["cp%d" % h], 1)
+    for blocks in CALLS:
         trs = []
-        for j in range(BPH):
-            q = h * BPH + j
+        for q in blocks:
+            g.wait_ge(sem["cp%d" % q], 1)
             r = relays[q]
+            lo = (q % 2) * W1_ENG
             trs.append(RemoteDMATransfer(dst_ids=[_dst(topo, r)],
-                                         dma_engine_mask=_pick(topo.mask(core, r), j * W1_ENG, W1_ENG),
-                                         remote_sem=sem.arr, src=T.part[:, q * BW:(q + 1) * BW],
+                                         dma_engine_mask=_pick(topo.mask(core, r), lo, W1_ENG),
+                                         remote_sem=sem.arr, src=T.part[:, _cols(q)],
                                          dst=T["land%d" % slot][:]))
             sent += W1_ENG
         g.remote_dma_fused(trs, local_sem=sem.sent)
@@ -132,26 +149,20 @@ def rank_program(g, core, T, topo):
     sent += _count(pmask)
 
     g.vector.wait_ge(sem.peer_in, _count(topo.mask(peer, core)))
-    for h in range(NHALF):
-        c = slice(h * HW, (h + 1) * HW)
-        g.vector.tensor_tensor(ps[h][:, 0:HW], ps[h][:, 0:HW], T.peer[:, c], AluOpType.add
-                               ).then_inc(sem["acc%d" % h], 1)
+    for q in range(NBLK):
+        g.vector.tensor_tensor(ps[q][:, 0:BW], ps[q][:, 0:BW], T.peer[:, _cols(q)], AluOpType.add
+                               ).then_inc(sem.acc, 1)
+    g.vector.wait_ge(sem.acc, NBLK)
     far_relays = _plan(T, topo, topo.chip(far[0]))[2]
     stq = [g.sync, g.scalar]
-    for h in range(NHALF):
-        c = slice(h * HW, (h + 1) * HW)
-        n = 0
-        for q in range(h * BPH, (h + 1) * BPH):
-            m = topo.mask(far_relays[q], local[0])
-            for d in local[1:]:
-                m &= topo.mask(far_relays[q], d)
-            n += _count(m)
-        g.vector.wait_ge(sem["acc%d" % h], 1)
-        g.vector.wait_ge(sem["rem%d" % h], n)
-        g.vector.tensor_tensor(T.out[:, c], ps[h][:, 0:HW], T.rem[:, c], AluOpType.add
-                               ).then_inc(sem["fin%d" % h], 1)
-        stq[h].wait_ge(sem["fin%d" % h], 1)
+    for h, blocks in enumerate(HALVES):
+        for q in blocks:
+            g.vector.wait_ge(sem["rem%d" % q], _count(_out_mask(topo, far_relays[q], local)))
+            g.vector.tensor_tensor(T.out[:, _cols(q)], ps[q][:, 0:BW], T.rem[:, _cols(q)], AluOpType.add
+                                   ).then_inc(sem["fin%d" % h], 1)
+        c = _span(blocks)
+        stq[h].wait_ge(sem["fin%d" % h], len(blocks))
         stq[h].dma_start(T.y[:, c], T.out[:, c]).then_inc(sem.st, 16)
 
     g.wait_ge(sem.sent, sent)
-    g.wait_ge(sem.st, 16 * NHALF)
+    g.wait_ge(sem.st, 16 * len(HALVES))

@@ -14,21 +14,29 @@ SCRATCH = {
     "al_s": ("sbuf", [128, 128], "bfloat16"),
     "bh_s": ("sbuf", [128, F], "bfloat16"),
     "bl_s": ("sbuf", [128, F], "bfloat16"),
+    "pah": ("sbuf", [128, 128], "bfloat16"),
+    "pal": ("sbuf", [128, 128], "bfloat16"),
+    "pbh": ("sbuf", [128, F], "bfloat16"),
+    "pbl": ("sbuf", [128, F], "bfloat16"),
     "ps0": ("psum", [128, 512], "float32"),
     "ps1": ("psum", [128, 512], "float32"),
     "ps2": ("psum", [128, 512], "float32"),
     "ps3": ("psum", [128, 512], "float32"),
+    "ps4": ("psum", [128, 512], "float32"),
+    "ps5": ("psum", [128, 512], "float32"),
+    "ps6": ("psum", [128, 512], "float32"),
+    "ps7": ("psum", [128, 512], "float32"),
     "part": ("sbuf", [128, F], "float32"),
-    "peer": ("sbuf", [128, F], "float32"),
     "rem": ("sbuf", [128, F], "float32"),
     "out": ("sbuf", [128, F], "float32"),
     "land0": ("sbuf", [128, BW], "float32"),
     "land1": ("sbuf", [128, BW], "float32"),
 }
-SEMAPHORES = (["lda", "sent", "arr", "peer_in", "acc", "st"]
+SEMAPHORES = (["lda", "sent", "arr", "pa_in", "acc", "st"]
               + ["ldh%d" % h for h in range(2)] + ["ldl%d" % h for h in range(2)] + ["fin%d" % h for h in range(2)]
+              + ["pb_in%d" % h for h in range(2)]
               + ["mm%d" % q for q in range(NBLK)] + ["cp%d" % q for q in range(NBLK)]
-              + ["rem%d" % q for q in range(NBLK)])
+              + ["pm%d" % q for q in range(NBLK)] + ["rem%d" % q for q in range(NBLK)])
 
 
 def _pick(mask, lo, n):
@@ -89,6 +97,16 @@ def _relay(g, core, T, topo, far, q):
     g.wait_ge(T.sem.sent, _count(mask))
 
 
+def _product(g, T, out, ah, al, bh, bl, q, first, last, sem):
+    c = _cols(q)
+    if first:
+        g.tensor.matmul(out[:, 0:BW], ah[:], bh[:, c], start=True, stop=False).then_inc(sem, 1)
+        g.tensor.matmul(out[:, 0:BW], al[:], bh[:, c], start=False, stop=False).then_inc(sem, 1)
+    if last:
+        g.tensor.matmul(out[:, 0:BW], ah[:], bl[:, c], start=False, stop=False).then_inc(sem, 1)
+        g.tensor.matmul(out[:, 0:BW], al[:], bl[:, c], start=False, stop=True).then_inc(sem, 1)
+
+
 def rank_program(g, core, T, topo):
     chips = sorted({topo.chip(c) for c in T.cores})
     if topo.chip(core) not in chips:
@@ -102,7 +120,16 @@ def rank_program(g, core, T, topo):
     slot = local.index(core)
     peer = local[1 - slot]
     ps = [T.ps0, T.ps1, T.ps2, T.ps3]
+    pp = [T.ps4, T.ps5, T.ps6, T.ps7]
     sem = T.sem
+    pmask = topo.mask(core, peer)
+
+    def to_peer(pairs, rsem):
+        g.remote_dma_fused(
+            [RemoteDMATransfer(dst_ids=[_dst(topo, peer)], dma_engine_mask=_pick(pmask, k * W1_ENG, W1_ENG),
+                               remote_sem=rsem, src=s, dst=d) for k, (d, s) in enumerate(pairs)],
+            local_sem=sem.sent)
+        return W1_ENG * len(pairs)
 
     g.sync.dma_start(T.ah_s[:], T.ah[:]).then_inc(sem.lda, 16)
     g.scalar.dma_start(T.al_s[:], T.al[:]).then_inc(sem.lda, 16)
@@ -115,22 +142,22 @@ def rank_program(g, core, T, topo):
     for h, blocks in enumerate(HALVES):
         g.tensor.wait_ge(sem["ldh%d" % h], 16)
         for q in blocks:
-            g.tensor.matmul(ps[q][:, 0:BW], T.ah_s[:], T.bh_s[:, _cols(q)], start=True, stop=False
-                            ).then_inc(sem["mm%d" % q], 1)
-            g.tensor.matmul(ps[q][:, 0:BW], T.al_s[:], T.bh_s[:, _cols(q)], start=False, stop=False
-                            ).then_inc(sem["mm%d" % q], 1)
+            _product(g, T, ps[q], T.ah_s, T.al_s, T.bh_s, T.bl_s, q, True, False, sem["mm%d" % q])
         g.tensor.wait_ge(sem["ldl%d" % h], 16)
         for q in blocks:
-            g.tensor.matmul(ps[q][:, 0:BW], T.ah_s[:], T.bl_s[:, _cols(q)], start=False, stop=False
-                            ).then_inc(sem["mm%d" % q], 1)
-            g.tensor.matmul(ps[q][:, 0:BW], T.al_s[:], T.bl_s[:, _cols(q)], start=False, stop=True
-                            ).then_inc(sem["mm%d" % q], 1)
+            _product(g, T, ps[q], T.ah_s, T.al_s, T.bh_s, T.bl_s, q, False, True, sem["mm%d" % q])
+    g.tensor.wait_ge(sem.pa_in, 2 * W1_ENG)
+    for h, blocks in enumerate(HALVES):
+        g.tensor.wait_ge(sem["pb_in%d" % h], 2 * W1_ENG)
+        for q in blocks:
+            _product(g, T, pp[q], T.pah, T.pal, T.pbh, T.pbl, q, True, True, sem["pm%d" % q])
 
     for q in range(NBLK):
         g.vector.wait_ge(sem["mm%d" % q], 4)
         g.vector.tensor_copy(T.part[:, _cols(q)], ps[q][:, 0:BW]).then_inc(sem["cp%d" % q], 1)
 
-    sent = 0
+    g.wait_ge(sem.lda, 32)
+    sent = to_peer([(T.pah[:], T.ah_s[:]), (T.pal[:], T.al_s[:])], sem.pa_in)
     for blocks in CALLS:
         trs = []
         for q in blocks:
@@ -143,14 +170,16 @@ def rank_program(g, core, T, topo):
                                          dst=T["land%d" % slot][:]))
             sent += W1_ENG
         g.remote_dma_fused(trs, local_sem=sem.sent)
-    rid, pid, _ = topo.addr(peer)
-    pmask = topo.mask(core, peer)
-    g.remote_dma(T.peer[:], T.part[:], sem.peer_in, sem.sent, pid, rid, pmask)
-    sent += _count(pmask)
+    for h, blocks in enumerate(HALVES):
+        c = _span(blocks)
+        g.wait_ge(sem["ldh%d" % h], 16)
+        g.wait_ge(sem["ldl%d" % h], 16)
+        sent += to_peer([(T.pbh[:, c], T.bh_s[:, c]), (T.pbl[:, c], T.bl_s[:, c])], sem["pb_in%d" % h])
 
-    g.vector.wait_ge(sem.peer_in, _count(topo.mask(peer, core)))
     for q in range(NBLK):
-        g.vector.tensor_tensor(ps[q][:, 0:BW], ps[q][:, 0:BW], T.peer[:, _cols(q)], AluOpType.add
+        g.vector.wait_ge(sem["cp%d" % q], 1)
+        g.vector.wait_ge(sem["pm%d" % q], 4)
+        g.vector.tensor_tensor(pp[q][:, 0:BW], pp[q][:, 0:BW], T.part[:, _cols(q)], AluOpType.add
                                ).then_inc(sem.acc, 1)
     g.vector.wait_ge(sem.acc, NBLK)
     far_relays = _plan(T, topo, topo.chip(far[0]))[2]
@@ -158,7 +187,7 @@ def rank_program(g, core, T, topo):
     for h, blocks in enumerate(HALVES):
         for q in blocks:
             g.vector.wait_ge(sem["rem%d" % q], _count(_out_mask(topo, far_relays[q], local)))
-            g.vector.tensor_tensor(T.out[:, _cols(q)], ps[q][:, 0:BW], T.rem[:, _cols(q)], AluOpType.add
+            g.vector.tensor_tensor(T.out[:, _cols(q)], pp[q][:, 0:BW], T.rem[:, _cols(q)], AluOpType.add
                                    ).then_inc(sem["fin%d" % h], 1)
         c = _span(blocks)
         stq[h].wait_ge(sem["fin%d" % h], len(blocks))

@@ -6,8 +6,10 @@ F = 512
 NBLK = 4
 BW = F // NBLK
 HALVES = [[0, 1], [2, 3]]
+STORES = [[0, 1], [2], [3]]
 CALLS = [[0], [1], [2, 3]]
 W1_ENG = 8
+AW = 64
 
 SCRATCH = {
     "ah_s": ("sbuf", [128, 128], "bfloat16"),
@@ -31,10 +33,11 @@ SCRATCH = {
     "out": ("sbuf", [128, F], "float32"),
     "land0": ("sbuf", [128, BW], "float32"),
     "land1": ("sbuf", [128, BW], "float32"),
+    "fa": ("sbuf", [128, AW], "bfloat16"),
 }
-SEMAPHORES = (["lda", "sent", "arr", "pa_in", "acc", "st"]
-              + ["ldh%d" % h for h in range(2)] + ["ldl%d" % h for h in range(2)] + ["fin%d" % h for h in range(2)]
-              + ["pb_in%d" % h for h in range(2)]
+SEMAPHORES = (["ldah", "ldal", "sent", "arr", "fa_in", "pal_in", "pah_in", "acc", "st"]
+              + ["ldh%d" % h for h in range(2)] + ["ldl%d" % h for h in range(2)]
+              + ["fin%d" % k for k in range(len(STORES))] + ["pb_in%d" % h for h in range(2)]
               + ["mm%d" % q for q in range(NBLK)] + ["cp%d" % q for q in range(NBLK)]
               + ["pm%d" % q for q in range(NBLK)] + ["rem%d" % q for q in range(NBLK)])
 
@@ -86,15 +89,22 @@ def _span(blocks):
     return slice(blocks[0] * BW, (blocks[-1] + 1) * BW)
 
 
-def _relay(g, core, T, topo, far, q):
+def _relay(g, core, T, topo, local, far, q):
     mask = _out_mask(topo, core, far)
+    n = _count(mask)
+    per = NBLK // len(local)
+    to = local[1 - q // per]
+    k = q % per
+    rid, pid, _ = topo.addr(to)
+    g.wait_ge(T.sem.fa_in, W1_ENG)
+    g.remote_dma(T.pal[:, k * AW:(k + 1) * AW], T.fa[:], T.sem.pal_in, T.sem.sent, pid, rid, mask)
     g.wait_ge(T.sem.arr, 2 * W1_ENG)
     g.remote_dma_fused(
         [RemoteDMATransfer(dst_ids=[_dst(topo, d) for d in far], dma_engine_mask=mask,
                            remote_sem=T.sem["rem%d" % q],
                            srcs=[T.land0[:], T.land1[:]], dsts=[T.rem[:, _cols(q)] for _ in far], alu_op=1)],
         local_sem=T.sem.sent)
-    g.wait_ge(T.sem.sent, _count(mask))
+    g.wait_ge(T.sem.sent, 2 * n)
 
 
 def _product(g, T, out, ah, al, bh, bl, q, first, last, sem):
@@ -113,7 +123,7 @@ def rank_program(g, core, T, topo):
         return
     local, far, relays = _plan(T, topo, topo.chip(core))
     if core in relays:
-        _relay(g, core, T, topo, far, relays.index(core))
+        _relay(g, core, T, topo, local, far, relays.index(core))
         return
     if T.rank_of(core) is None:
         return
@@ -123,22 +133,17 @@ def rank_program(g, core, T, topo):
     pp = [T.ps4, T.ps5, T.ps6, T.ps7]
     sem = T.sem
     pmask = topo.mask(core, peer)
+    per = NBLK // len(local)
 
-    def to_peer(pairs, rsem):
-        g.remote_dma_fused(
-            [RemoteDMATransfer(dst_ids=[_dst(topo, peer)], dma_engine_mask=_pick(pmask, k * W1_ENG, W1_ENG),
-                               remote_sem=rsem, src=s, dst=d) for k, (d, s) in enumerate(pairs)],
-            local_sem=sem.sent)
-        return W1_ENG * len(pairs)
-
-    g.sync.dma_start(T.ah_s[:], T.ah[:]).then_inc(sem.lda, 16)
-    g.scalar.dma_start(T.al_s[:], T.al[:]).then_inc(sem.lda, 16)
+    g.sync.dma_start(T.al_s[:], T.al[:]).then_inc(sem.ldal, 16)
+    g.scalar.dma_start(T.ah_s[:], T.ah[:]).then_inc(sem.ldah, 16)
     for h, blocks in enumerate(HALVES):
         c = _span(blocks)
         g.sync.dma_start(T.bh_s[:, c], T.bh[:, c]).then_inc(sem["ldh%d" % h], 16)
         g.scalar.dma_start(T.bl_s[:, c], T.bl[:, c]).then_inc(sem["ldl%d" % h], 16)
 
-    g.tensor.wait_ge(sem.lda, 32)
+    g.tensor.wait_ge(sem.ldal, 16)
+    g.tensor.wait_ge(sem.ldah, 16)
     for h, blocks in enumerate(HALVES):
         g.tensor.wait_ge(sem["ldh%d" % h], 16)
         for q in blocks:
@@ -146,7 +151,9 @@ def rank_program(g, core, T, topo):
         g.tensor.wait_ge(sem["ldl%d" % h], 16)
         for q in blocks:
             _product(g, T, ps[q], T.ah_s, T.al_s, T.bh_s, T.bl_s, q, False, True, sem["mm%d" % q])
-    g.tensor.wait_ge(sem.pa_in, 2 * W1_ENG)
+    mine = [relays[(1 - slot) * per + k] for k in range(per)]
+    g.tensor.wait_ge(sem.pal_in, sum(_count(_out_mask(topo, r, far)) for r in mine))
+    g.tensor.wait_ge(sem.pah_in, _count(topo.mask(peer, core)))
     for h, blocks in enumerate(HALVES):
         g.tensor.wait_ge(sem["pb_in%d" % h], 2 * W1_ENG)
         for q in blocks:
@@ -156,8 +163,14 @@ def rank_program(g, core, T, topo):
         g.vector.wait_ge(sem["mm%d" % q], 4)
         g.vector.tensor_copy(T.part[:, _cols(q)], ps[q][:, 0:BW]).then_inc(sem["cp%d" % q], 1)
 
-    g.wait_ge(sem.lda, 32)
-    sent = to_peer([(T.pah[:], T.ah_s[:]), (T.pal[:], T.al_s[:])], sem.pa_in)
+    g.wait_ge(sem.ldal, 16)
+    g.remote_dma_fused(
+        [RemoteDMATransfer(dst_ids=[_dst(topo, relays[slot * per + k])],
+                           dma_engine_mask=_pick(topo.mask(core, relays[slot * per + k]), k * W1_ENG, W1_ENG),
+                           remote_sem=sem.fa_in, src=T.al_s[:, k * AW:(k + 1) * AW], dst=T.fa[:])
+         for k in range(per)],
+        local_sem=sem.sent)
+    sent = per * W1_ENG
     for blocks in CALLS:
         trs = []
         for q in blocks:
@@ -170,11 +183,20 @@ def rank_program(g, core, T, topo):
                                          dst=T["land%d" % slot][:]))
             sent += W1_ENG
         g.remote_dma_fused(trs, local_sem=sem.sent)
+    rid, pid, _ = topo.addr(peer)
+    g.wait_ge(sem.ldah, 16)
+    g.remote_dma(T.pah[:], T.ah_s[:], sem.pah_in, sem.sent, pid, rid, pmask)
+    sent += _count(pmask)
     for h, blocks in enumerate(HALVES):
         c = _span(blocks)
         g.wait_ge(sem["ldh%d" % h], 16)
         g.wait_ge(sem["ldl%d" % h], 16)
-        sent += to_peer([(T.pbh[:, c], T.bh_s[:, c]), (T.pbl[:, c], T.bl_s[:, c])], sem["pb_in%d" % h])
+        g.remote_dma_fused(
+            [RemoteDMATransfer(dst_ids=[_dst(topo, peer)], dma_engine_mask=_pick(pmask, k * W1_ENG, W1_ENG),
+                               remote_sem=sem["pb_in%d" % h], src=s, dst=d)
+             for k, (d, s) in enumerate([(T.pbh[:, c], T.bh_s[:, c]), (T.pbl[:, c], T.bl_s[:, c])])],
+            local_sem=sem.sent)
+        sent += 2 * W1_ENG
 
     for q in range(NBLK):
         g.vector.wait_ge(sem["cp%d" % q], 1)
@@ -184,14 +206,14 @@ def rank_program(g, core, T, topo):
     g.vector.wait_ge(sem.acc, NBLK)
     far_relays = _plan(T, topo, topo.chip(far[0]))[2]
     stq = [g.sync, g.scalar]
-    for h, blocks in enumerate(HALVES):
+    for k, blocks in enumerate(STORES):
         for q in blocks:
             g.vector.wait_ge(sem["rem%d" % q], _count(_out_mask(topo, far_relays[q], local)))
             g.vector.tensor_tensor(T.out[:, _cols(q)], pp[q][:, 0:BW], T.rem[:, _cols(q)], AluOpType.add
-                                   ).then_inc(sem["fin%d" % h], 1)
+                                   ).then_inc(sem["fin%d" % k], 1)
         c = _span(blocks)
-        stq[h].wait_ge(sem["fin%d" % h], len(blocks))
-        stq[h].dma_start(T.y[:, c], T.out[:, c]).then_inc(sem.st, 16)
+        stq[k % 2].wait_ge(sem["fin%d" % k], len(blocks))
+        stq[k % 2].dma_start(T.y[:, c], T.out[:, c]).then_inc(sem.st, 16)
 
     g.wait_ge(sem.sent, sent)
-    g.wait_ge(sem.st, 16 * len(HALVES))
+    g.wait_ge(sem.st, 16 * len(STORES))

from concourse.bass import DstId, RemoteDMATransfer
from concourse.mybir import AluOpType

NSIM = 96
F = 512
NBLK = 4
BW = F // NBLK
HALVES = [[0, 1], [2, 3]]
STORES = [[0, 1], [2], [3]]
CALLS = [[0], [1], [2, 3]]
W1_ENG = 8
AW = 64

SCRATCH = {
    "ah_s": ("sbuf", [128, 128], "bfloat16"),
    "al_s": ("sbuf", [128, 128], "bfloat16"),
    "bh_s": ("sbuf", [128, F], "bfloat16"),
    "bl_s": ("sbuf", [128, F], "bfloat16"),
    "pah": ("sbuf", [128, 128], "bfloat16"),
    "pal": ("sbuf", [128, 128], "bfloat16"),
    "pbh": ("sbuf", [128, F], "bfloat16"),
    "pbl": ("sbuf", [128, F], "bfloat16"),
    "ps0": ("psum", [128, 512], "float32"),
    "ps1": ("psum", [128, 512], "float32"),
    "ps2": ("psum", [128, 512], "float32"),
    "ps3": ("psum", [128, 512], "float32"),
    "ps4": ("psum", [128, 512], "float32"),
    "ps5": ("psum", [128, 512], "float32"),
    "ps6": ("psum", [128, 512], "float32"),
    "ps7": ("psum", [128, 512], "float32"),
    "part": ("sbuf", [128, F], "float32"),
    "rem": ("sbuf", [128, F], "float32"),
    "out": ("sbuf", [128, F], "float32"),
    "land0": ("sbuf", [128, BW], "float32"),
    "land1": ("sbuf", [128, BW], "float32"),
    "fa": ("sbuf", [128, AW], "bfloat16"),
}
SEMAPHORES = (["ldah", "ldal", "sent", "arr", "fa_in", "pal_in", "pah_in", "acc", "st"]
              + ["ldh%d" % h for h in range(2)] + ["ldl%d" % h for h in range(2)]
              + ["fin%d" % k for k in range(len(STORES))] + ["pb_in%d" % h for h in range(2)]
              + ["mm%d" % q for q in range(NBLK)] + ["cp%d" % q for q in range(NBLK)]
              + ["pm%d" % q for q in range(NBLK)] + ["rem%d" % q for q in range(NBLK)])


def _pick(mask, lo, n):
    bits = [i for i in range(mask.bit_length()) if (mask >> i) & 1]
    m = 0
    for b in bits[lo:lo + n]:
        m |= 1 << b
    return m


def _count(mask):
    return sum((mask >> i) & 1 for i in range(mask.bit_length()))


def _plan(T, topo, chip):
    local = [c for c in T.cores if topo.chip(c) == chip]
    far = [c for c in T.cores if topo.chip(c) != chip]
    by_die = {}
    for c in range(NSIM):
        if topo.chip(c) == chip and c not in T.cores and all(topo.may_write(c, d) for d in far):
            by_die.setdefault(topo.die(c), []).append(c)
    relays = []
    for i in range(max(len(v) for v in by_die.values())):
        for d in sorted(by_die):
            if i < len(by_die[d]):
                relays.append(by_die[d][i])
    return local, far, relays[:NBLK]


def _out_mask(topo, src, dsts):
    m = topo.mask(src, dsts[0])
    for d in dsts[1:]:
        m &= topo.mask(src, d)
    return m


def _dst(topo, c):
    rid, pid, _ = topo.addr(c)
    return DstId(rid=rid, pnc=pid)


def _cols(q):
    return slice(q * BW, (q + 1) * BW)


def _span(blocks):
    return slice(blocks[0] * BW, (blocks[-1] + 1) * BW)


def _relay(g, core, T, topo, local, far, q):
    mask = _out_mask(topo, core, far)
    n = _count(mask)
    per = NBLK // len(local)
    to = local[1 - q // per]
    k = q % per
    rid, pid, _ = topo.addr(to)
    g.wait_ge(T.sem.fa_in, W1_ENG)
    g.remote_dma(T.pal[:, k * AW:(k + 1) * AW], T.fa[:], T.sem.pal_in, T.sem.sent, pid, rid, mask)
    g.wait_ge(T.sem.arr, 2 * W1_ENG)
    g.remote_dma_fused(
        [RemoteDMATransfer(dst_ids=[_dst(topo, d) for d in far], dma_engine_mask=mask,
                           remote_sem=T.sem["rem%d" % q],
                           srcs=[T.land0[:], T.land1[:]], dsts=[T.rem[:, _cols(q)] for _ in far], alu_op=1)],
        local_sem=T.sem.sent)
    g.wait_ge(T.sem.sent, 2 * n)


def _product(g, T, out, ah, al, bh, bl, q, first, last, sem):
    c = _cols(q)
    if first:
        g.tensor.matmul(out[:, 0:BW], ah[:], bh[:, c], start=True, stop=False).then_inc(sem, 1)
        g.tensor.matmul(out[:, 0:BW], al[:], bh[:, c], start=False, stop=False).then_inc(sem, 1)
    if last:
        g.tensor.matmul(out[:, 0:BW], ah[:], bl[:, c], start=False, stop=False).then_inc(sem, 1)
        g.tensor.matmul(out[:, 0:BW], al[:], bl[:, c], start=False, stop=True).then_inc(sem, 1)


def rank_program(g, core, T, topo):
    chips = sorted({topo.chip(c) for c in T.cores})
    if topo.chip(core) not in chips:
        return
    local, far, relays = _plan(T, topo, topo.chip(core))
    if core in relays:
        _relay(g, core, T, topo, local, far, relays.index(core))
        return
    if T.rank_of(core) is None:
        return
    slot = local.index(core)
    peer = local[1 - slot]
    ps = [T.ps0, T.ps1, T.ps2, T.ps3]
    pp = [T.ps4, T.ps5, T.ps6, T.ps7]
    sem = T.sem
    pmask = topo.mask(core, peer)
    per = NBLK // len(local)

    g.sync.dma_start(T.al_s[:], T.al[:]).then_inc(sem.ldal, 16)
    g.scalar.dma_start(T.ah_s[:], T.ah[:]).then_inc(sem.ldah, 16)
    for h, blocks in enumerate(HALVES):
        c = _span(blocks)
        g.sync.dma_start(T.bh_s[:, c], T.bh[:, c]).then_inc(sem["ldh%d" % h], 16)
        g.scalar.dma_start(T.bl_s[:, c], T.bl[:, c]).then_inc(sem["ldl%d" % h], 16)

    g.tensor.wait_ge(sem.ldal, 16)
    g.tensor.wait_ge(sem.ldah, 16)
    for h, blocks in enumerate(HALVES):
        g.tensor.wait_ge(sem["ldh%d" % h], 16)
        for q in blocks:
            _product(g, T, ps[q], T.ah_s, T.al_s, T.bh_s, T.bl_s, q, True, False, sem["mm%d" % q])
        g.tensor.wait_ge(sem["ldl%d" % h], 16)
        for q in blocks:
            _product(g, T, ps[q], T.ah_s, T.al_s, T.bh_s, T.bl_s, q, False, True, sem["mm%d" % q])
    mine = [relays[(1 - slot) * per + k] for k in range(per)]
    g.tensor.wait_ge(sem.pal_in, sum(_count(_out_mask(topo, r, far)) for r in mine))
    g.tensor.wait_ge(sem.pah_in, _count(topo.mask(peer, core)))
    for h, blocks in enumerate(HALVES):
        g.tensor.wait_ge(sem["pb_in%d" % h], 2 * W1_ENG)
        for q in blocks:
            _product(g, T, pp[q], T.pah, T.pal, T.pbh, T.pbl, q, True, True, sem["pm%d" % q])

    for q in range(NBLK):
        g.vector.wait_ge(sem["mm%d" % q], 4)
        g.vector.tensor_copy(T.part[:, _cols(q)], ps[q][:, 0:BW]).then_inc(sem["cp%d" % q], 1)

    g.wait_ge(sem.ldal, 16)
    g.remote_dma_fused(
        [RemoteDMATransfer(dst_ids=[_dst(topo, relays[slot * per + k])],
                           dma_engine_mask=_pick(topo.mask(core, relays[slot * per + k]), k * W1_ENG, W1_ENG),
                           remote_sem=sem.fa_in, src=T.al_s[:, k * AW:(k + 1) * AW], dst=T.fa[:])
         for k in range(per)],
        local_sem=sem.sent)
    sent = per * W1_ENG
    for blocks in CALLS:
        trs = []
        for q in blocks:
            g.wait_ge(sem["cp%d" % q], 1)
            r = relays[q]
            lo = (q % 2) * W1_ENG
            trs.append(RemoteDMATransfer(dst_ids=[_dst(topo, r)],
                                         dma_engine_mask=_pick(topo.mask(core, r), lo, W1_ENG),
                                         remote_sem=sem.arr, src=T.part[:, _cols(q)],
                                         dst=T["land%d" % slot][:]))
            sent += W1_ENG
        g.remote_dma_fused(trs, local_sem=sem.sent)
    rid, pid, _ = topo.addr(peer)
    g.wait_ge(sem.ldah, 16)
    g.remote_dma(T.pah[:], T.ah_s[:], sem.pah_in, sem.sent, pid, rid, pmask)
    sent += _count(pmask)
    for h, blocks in enumerate(HALVES):
        c = _span(blocks)
        g.wait_ge(sem["ldh%d" % h], 16)
        g.wait_ge(sem["ldl%d" % h], 16)
        g.remote_dma_fused(
            [RemoteDMATransfer(dst_ids=[_dst(topo, peer)], dma_engine_mask=_pick(pmask, k * W1_ENG, W1_ENG),
                               remote_sem=sem["pb_in%d" % h], src=s, dst=d)
             for k, (d, s) in enumerate([(T.pbh[:, c], T.bh_s[:, c]), (T.pbl[:, c], T.bl_s[:, c])])],
            local_sem=sem.sent)
        sent += 2 * W1_ENG

    for q in range(NBLK):
        g.vector.wait_ge(sem["cp%d" % q], 1)
        g.vector.wait_ge(sem["pm%d" % q], 4)
        g.vector.tensor_tensor(pp[q][:, 0:BW], pp[q][:, 0:BW], T.part[:, _cols(q)], AluOpType.add
                               ).then_inc(sem.acc, 1)
    g.vector.wait_ge(sem.acc, NBLK)
    far_relays = _plan(T, topo, topo.chip(far[0]))[2]
    stq = [g.sync, g.scalar]
    for k, blocks in enumerate(STORES):
        for q in blocks:
            g.vector.wait_ge(sem["rem%d" % q], _count(_out_mask(topo, far_relays[q], local)))
            g.vector.tensor_tensor(T.out[:, _cols(q)], pp[q][:, 0:BW], T.rem[:, _cols(q)], AluOpType.add
                                   ).then_inc(sem["fin%d" % k], 1)
        c = _span(blocks)
        stq[k % 2].wait_ge(sem["fin%d" % k], len(blocks))
        stq[k % 2].dma_start(T.y[:, c], T.out[:, c]).then_inc(sem.st, 16)

    g.wait_ge(sem.sent, sent)
    g.wait_ge(sem.st, 16 * len(STORES))
